import numpy as np
import ml_dtypes

BF16 = ml_dtypes.bfloat16


def bf(x):
    return np.asarray(x, np.float32).astype(BF16)


def f32(x):
    return np.asarray(x, np.float32)


def f64(x):
    return np.asarray(x).astype(np.float64)


def striped(idx):
    return np.tile(idx.reshape(-1, 16).T, (8, 1))


S, K, M, N = 4096, 256, 128, 4096


def setup_inputs():
    return {"table": bf(np.random.standard_normal((K, S))), "w": bf(np.random.standard_normal((K, M)) / np.sqrt(K)), "b": f32(0.5 * np.random.standard_normal((M, 1))), "offs": striped(np.random.permutation(S))}


def reference(table, w, b, offs):
    idx = offs[:16].T.reshape(-1)
    x = f64(table)[:, idx]
    y = f64(w).T @ x
    return np.maximum(y + f64(b), 0.0)

@@ -1,0 +1,51 @@
+import concourse.mybir as mybir
+
+BF16, F32, U16 = mybir.dt.bfloat16, mybir.dt.float32, mybir.dt.uint16
+
+P = 128
+K, S, M, N = 256, 4096, 128, 4096
+K_BLOCKS = K // P
+PIECE = 512
+PIECES = N // PIECE
+PIECE_COLS = PIECE // 16
+
+FLOPS = 2 * K * M * N
+
+
+def tile_gather_matmul_kernel(tc, table, w, b, offs, out):
+    nc = tc.nc
+    with (
+        tc.tile_pool(name="held", bufs=1) as held,
+        tc.psum_pool(name="psum", bufs=1) as psum,
+    ):
+        offsets = held.tile([P, N // 16], U16, name="offsets")
+        nc.sync.dma_start(offsets[:], offs)
+        weights = held.tile([P, K_BLOCKS, M], BF16, name="weights")
+        nc.sync.dma_start(weights[:], w.rearrange("(a p) m -> p a m", p=P))
+        bias = held.tile([P, 1], F32, name="bias")
+        nc.sync.dma_start(bias[:], b)
+        blocks = [held.tile([P, S], BF16, name=f"block{a}") for a in range(K_BLOCKS)]
+        for a in range(K_BLOCKS):
+            nc.scalar.dma_start(blocks[a][:], table[a * P : (a + 1) * P, :])
+
+        banks = [psum.tile([P, PIECE], F32, name=f"bank{i}") for i in range(PIECES)]
+        result = held.tile([P, N], F32, name="result")
+        for a in range(K_BLOCKS):
+            for i in range(PIECES):
+                picked = blocks[a][:].indirect(offsets[:, i * PIECE_COLS : (i + 1) * PIECE_COLS])
+                nc.tensor.matmul(
+                    banks[i][:], weights[:, a, :], picked, start=(a == 0), stop=(a == K_BLOCKS - 1)
+                )
+
+        for i in range(PIECES):
+            columns = slice(i * PIECE, (i + 1) * PIECE)
+            if i % 2 == 0:
+                nc.vector.tensor_scalar(
+                    result[:, columns], banks[i][:], bias[:, 0:1], 0.0,
+                    op0=mybir.AluOpType.add, op1=mybir.AluOpType.max,
+                )
+            else:
+                nc.scalar.activation(
+                    result[:, columns], banks[i][:], mybir.ActivationFunctionType.Relu, bias=bias[:, 0:1]
+                )
+            nc.sync.dma_start(out[:, columns], result[:, columns])

@@ -30,12 +30,15 @@ def tile_gather_matmul_kernel(tc, table, w, b, offs, out):
 
         banks = [psum.tile([P, PIECE], F32, name=f"bank{i}") for i in range(PIECES)]
         result = held.tile([P, N], F32, name="result")
-        for a in range(K_BLOCKS):
-            for i in range(PIECES):
-                picked = blocks[a][:].indirect(offsets[:, i * PIECE_COLS : (i + 1) * PIECE_COLS])
-                nc.tensor.matmul(
-                    banks[i][:], weights[:, a, :], picked, start=(a == 0), stop=(a == K_BLOCKS - 1)
-                )
+        early = range(PIECES // 2)
+        late = range(PIECES // 2, PIECES)
+        order = [(a, i) for a in range(K_BLOCKS) for i in early]
+        order += [(a, i) for i in late for a in range(K_BLOCKS)]
+        for a, i in order:
+            picked = blocks[a][:].indirect(offsets[:, i * PIECE_COLS : (i + 1) * PIECE_COLS])
+            nc.tensor.matmul(
+                banks[i][:], weights[:, a, :], picked, start=(a == 0), stop=(a == K_BLOCKS - 1)
+            )
 
         for i in range(PIECES):
             columns = slice(i * PIECE, (i + 1) * PIECE)

@@ -8,6 +8,7 @@ K_BLOCKS = K // P
 PIECE = 512
 PIECES = N // PIECE
 PIECE_COLS = PIECE // 16
+WARM_UPS = 8
 
 FLOPS = 2 * K * M * N
 
@@ -28,17 +29,19 @@ def tile_gather_matmul_kernel(tc, table, w, b, offs, out):
         for a in range(K_BLOCKS):
             nc.scalar.dma_start(blocks[a][:], table[a * P : (a + 1) * P, :])
 
+        zeros = held.tile([P, PIECE], BF16, name="zeros")
+        nc.vector.memset(zeros[:], 0.0)
+
         banks = [psum.tile([P, PIECE], F32, name=f"bank{i}") for i in range(PIECES)]
         result = held.tile([P, N], F32, name="result")
-        early = range(PIECES // 2)
-        late = range(PIECES // 2, PIECES)
-        order = [(a, i) for a in range(K_BLOCKS) for i in early]
-        order += [(a, i) for i in late for a in range(K_BLOCKS)]
-        for a, i in order:
-            picked = blocks[a][:].indirect(offsets[:, i * PIECE_COLS : (i + 1) * PIECE_COLS])
-            nc.tensor.matmul(
-                banks[i][:], weights[:, a, :], picked, start=(a == 0), stop=(a == K_BLOCKS - 1)
-            )
+        for turn in range(WARM_UPS):
+            nc.tensor.matmul(banks[PIECES - 1][:], zeros[:, 0:M], zeros[:], start=True, stop=True)
+        for a in range(K_BLOCKS):
+            for i in range(PIECES):
+                picked = blocks[a][:].indirect(offsets[:, i * PIECE_COLS : (i + 1) * PIECE_COLS])
+                nc.tensor.matmul(
+                    banks[i][:], weights[:, a, :], picked, start=(a == 0), stop=(a == K_BLOCKS - 1)
+                )
 
         for i in range(PIECES):
             columns = slice(i * PIECE, (i + 1) * PIECE)

@@ -8,7 +8,7 @@ K_BLOCKS = K // P
 PIECE = 512
 PIECES = N // PIECE
 PIECE_COLS = PIECE // 16
-WARM_UPS = 8
+EARLY = 4
 
 FLOPS = 2 * K * M * N
 
@@ -17,7 +17,7 @@ def tile_gather_matmul_kernel(tc, table, w, b, offs, out):
     nc = tc.nc
     with (
         tc.tile_pool(name="held", bufs=1) as held,
-        tc.psum_pool(name="psum", bufs=1) as psum,
+        tc.psum_pool(name="psum", bufs=EARLY) as psum,
     ):
         offsets = held.tile([P, N // 16], U16, name="offsets")
         nc.sync.dma_start(offsets[:], offs)
@@ -28,30 +28,35 @@ def tile_gather_matmul_kernel(tc, table, w, b, offs, out):
         blocks = [held.tile([P, S], BF16, name=f"block{a}") for a in range(K_BLOCKS)]
         for a in range(K_BLOCKS):
             nc.scalar.dma_start(blocks[a][:], table[a * P : (a + 1) * P, :])
-
-        zeros = held.tile([P, PIECE], BF16, name="zeros")
-        nc.vector.memset(zeros[:], 0.0)
-
-        banks = [psum.tile([P, PIECE], F32, name=f"bank{i}") for i in range(PIECES)]
         result = held.tile([P, N], F32, name="result")
-        for turn in range(WARM_UPS):
-            nc.tensor.matmul(banks[PIECES - 1][:], zeros[:, 0:M], zeros[:], start=True, stop=True)
-        for a in range(K_BLOCKS):
-            for i in range(PIECES):
-                picked = blocks[a][:].indirect(offsets[:, i * PIECE_COLS : (i + 1) * PIECE_COLS])
-                nc.tensor.matmul(
-                    banks[i][:], weights[:, a, :], picked, start=(a == 0), stop=(a == K_BLOCKS - 1)
-                )
 
-        for i in range(PIECES):
+        def multiply(bank, a, i):
+            picked = blocks[a][:].indirect(offsets[:, i * PIECE_COLS : (i + 1) * PIECE_COLS])
+            nc.tensor.matmul(
+                bank[:], weights[:, a, :], picked, start=(a == 0), stop=(a == K_BLOCKS - 1)
+            )
+
+        def finish(bank, i):
             columns = slice(i * PIECE, (i + 1) * PIECE)
             if i % 2 == 0:
                 nc.vector.tensor_scalar(
-                    result[:, columns], banks[i][:], bias[:, 0:1], 0.0,
+                    result[:, columns], bank[:], bias[:, 0:1], 0.0,
                     op0=mybir.AluOpType.add, op1=mybir.AluOpType.max,
                 )
             else:
                 nc.scalar.activation(
-                    result[:, columns], banks[i][:], mybir.ActivationFunctionType.Relu, bias=bias[:, 0:1]
+                    result[:, columns], bank[:], mybir.ActivationFunctionType.Relu, bias=bias[:, 0:1]
                 )
             nc.sync.dma_start(out[:, columns], result[:, columns])
+
+        early_banks = [psum.tile([P, PIECE], F32, name="bank") for i in range(EARLY)]
+        for i in range(EARLY):
+            multiply(early_banks[i], 0, i)
+        for i in range(EARLY):
+            multiply(early_banks[i], 1, i)
+            finish(early_banks[i], i)
+        for i in range(EARLY, PIECES):
+            bank = psum.tile([P, PIECE], F32, name="bank")
+            for a in range(K_BLOCKS):
+                multiply(bank, a, i)
+            finish(bank, i)

@@ -36,27 +36,31 @@ def tile_gather_matmul_kernel(tc, table, w, b, offs, out):
                 bank[:], weights[:, a, :], picked, start=(a == 0), stop=(a == K_BLOCKS - 1)
             )
 
-        def finish(bank, i):
-            columns = slice(i * PIECE, (i + 1) * PIECE)
-            if i % 2 == 0:
-                nc.vector.tensor_scalar(
-                    result[:, columns], bank[:], bias[:, 0:1], 0.0,
-                    op0=mybir.AluOpType.add, op1=mybir.AluOpType.max,
-                )
-            else:
-                nc.scalar.activation(
-                    result[:, columns], bank[:], mybir.ActivationFunctionType.Relu, bias=bias[:, 0:1]
-                )
-            nc.sync.dma_start(out[:, columns], result[:, columns])
+        def finish(bank, i, parts):
+            width = PIECE // parts
+            for part in range(parts):
+                inside = slice(part * width, (part + 1) * width)
+                columns = slice(i * PIECE + part * width, i * PIECE + (part + 1) * width)
+                if i % 2 == 0:
+                    nc.vector.tensor_scalar(
+                        result[:, columns], bank[:, inside], bias[:, 0:1], 0.0,
+                        op0=mybir.AluOpType.add, op1=mybir.AluOpType.max,
+                    )
+                else:
+                    nc.scalar.activation(
+                        result[:, columns], bank[:, inside],
+                        mybir.ActivationFunctionType.Relu, bias=bias[:, 0:1],
+                    )
+                nc.sync.dma_start(out[:, columns], result[:, columns])
 
         early_banks = [psum.tile([P, PIECE], F32, name="bank") for i in range(EARLY)]
         for i in range(EARLY):
             multiply(early_banks[i], 0, i)
         for i in range(EARLY):
             multiply(early_banks[i], 1, i)
-            finish(early_banks[i], i)
+            finish(early_banks[i], i, parts=1)
         for i in range(EARLY, PIECES):
             bank = psum.tile([P, PIECE], F32, name="bank")
             for a in range(K_BLOCKS):
                 multiply(bank, a, i)
-            finish(bank, i)
+            finish(bank, i, parts=(2 if i == PIECES - 1 else 1))

@@ -21,13 +21,13 @@ def tile_gather_matmul_kernel(tc, table, w, b, offs, out):
     ):
         offsets = held.tile([P, N // 16], U16, name="offsets")
         nc.sync.dma_start(offsets[:], offs)
-        weights = held.tile([P, K_BLOCKS, M], BF16, name="weights")
-        nc.sync.dma_start(weights[:], w.rearrange("(a p) m -> p a m", p=P))
-        bias = held.tile([P, 1], F32, name="bias")
-        nc.sync.dma_start(bias[:], b)
         blocks = [held.tile([P, S], BF16, name=f"block{a}") for a in range(K_BLOCKS)]
         for a in range(K_BLOCKS):
-            nc.scalar.dma_start(blocks[a][:], table[a * P : (a + 1) * P, :])
+            nc.sync.dma_start(blocks[a][:], table[a * P : (a + 1) * P, :])
+        weights = held.tile([P, K_BLOCKS, M], BF16, name="weights")
+        nc.scalar.dma_start(weights[:], w.rearrange("(a p) m -> p a m", p=P))
+        bias = held.tile([P, 1], F32, name="bias")
+        nc.scalar.dma_start(bias[:], b)
         result = held.tile([P, N], F32, name="result")
 
         def multiply(bank, a, i):

@@ -41,7 +41,7 @@ def tile_gather_matmul_kernel(tc, table, w, b, offs, out):
             for part in range(parts):
                 inside = slice(part * width, (part + 1) * width)
                 columns = slice(i * PIECE + part * width, i * PIECE + (part + 1) * width)
-                if i % 2 == 0:
+                if i % 2 == 1:
                     nc.vector.tensor_scalar(
                         result[:, columns], bank[:, inside], bias[:, 0:1], 0.0,
                         op0=mybir.AluOpType.add, op1=mybir.AluOpType.max,

@@ -8,6 +8,7 @@ K_BLOCKS = K // P
 PIECE = 512
 PIECES = N // PIECE
 PIECE_COLS = PIECE // 16
+LINE = 256
 EARLY = 4
 
 FLOPS = 2 * K * M * N
@@ -19,16 +20,18 @@ def tile_gather_matmul_kernel(tc, table, w, b, offs, out):
         tc.tile_pool(name="held", bufs=1) as held,
         tc.psum_pool(name="psum", bufs=EARLY) as psum,
     ):
-        offsets = held.tile([P, N // 16], U16, name="offsets")
+        offsets = held.tile([P, N // 16], U16, name="offsets", align_bytes=LINE)
         nc.sync.dma_start(offsets[:], offs)
-        blocks = [held.tile([P, S], BF16, name=f"block{a}") for a in range(K_BLOCKS)]
+        blocks = [
+            held.tile([P, S], BF16, name=f"block{a}", align_bytes=LINE) for a in range(K_BLOCKS)
+        ]
         for a in range(K_BLOCKS):
             nc.sync.dma_start(blocks[a][:], table[a * P : (a + 1) * P, :])
-        weights = held.tile([P, K_BLOCKS, M], BF16, name="weights")
+        weights = held.tile([P, K_BLOCKS, M], BF16, name="weights", align_bytes=LINE)
         nc.scalar.dma_start(weights[:], w.rearrange("(a p) m -> p a m", p=P))
         bias = held.tile([P, 1], F32, name="bias")
         nc.scalar.dma_start(bias[:], b)
-        result = held.tile([P, N], F32, name="result")
+        result = held.tile([P, N], F32, name="result", align_bytes=LINE)
 
         def multiply(bank, a, i):
             picked = blocks[a][:].indirect(offsets[:, i * PIECE_COLS : (i + 1) * PIECE_COLS])

import concourse.mybir as mybir

BF16, F32, U16 = mybir.dt.bfloat16, mybir.dt.float32, mybir.dt.uint16

P = 128
K, S, M, N = 256, 4096, 128, 4096
K_BLOCKS = K // P
PIECE = 512
PIECES = N // PIECE
PIECE_COLS = PIECE // 16
LINE = 256
EARLY = 4

FLOPS = 2 * K * M * N


def tile_gather_matmul_kernel(tc, table, w, b, offs, out):
    nc = tc.nc
    with (
        tc.tile_pool(name="held", bufs=1) as held,
        tc.psum_pool(name="psum", bufs=EARLY) as psum,
    ):
        offsets = held.tile([P, N // 16], U16, name="offsets", align_bytes=LINE)
        nc.sync.dma_start(offsets[:], offs)
        blocks = [
            held.tile([P, S], BF16, name=f"block{a}", align_bytes=LINE) for a in range(K_BLOCKS)
        ]
        for a in range(K_BLOCKS):
            nc.sync.dma_start(blocks[a][:], table[a * P : (a + 1) * P, :])
        weights = held.tile([P, K_BLOCKS, M], BF16, name="weights", align_bytes=LINE)
        nc.scalar.dma_start(weights[:], w.rearrange("(a p) m -> p a m", p=P))
        bias = held.tile([P, 1], F32, name="bias")
        nc.scalar.dma_start(bias[:], b)
        result = held.tile([P, N], F32, name="result", align_bytes=LINE)

        def multiply(bank, a, i):
            picked = blocks[a][:].indirect(offsets[:, i * PIECE_COLS : (i + 1) * PIECE_COLS])
            nc.tensor.matmul(
                bank[:], weights[:, a, :], picked, start=(a == 0), stop=(a == K_BLOCKS - 1)
            )

        def finish(bank, i, parts):
            width = PIECE // parts
            for part in range(parts):
                inside = slice(part * width, (part + 1) * width)
                columns = slice(i * PIECE + part * width, i * PIECE + (part + 1) * width)
                if i % 2 == 1:
                    nc.vector.tensor_scalar(
                        result[:, columns], bank[:, inside], bias[:, 0:1], 0.0,
                        op0=mybir.AluOpType.add, op1=mybir.AluOpType.max,
                    )
                else:
                    nc.scalar.activation(
                        result[:, columns], bank[:, inside],
                        mybir.ActivationFunctionType.Relu, bias=bias[:, 0:1],
                    )
                nc.sync.dma_start(out[:, columns], result[:, columns])

        early_banks = [psum.tile([P, PIECE], F32, name="bank") for i in range(EARLY)]
        for i in range(EARLY):
            multiply(early_banks[i], 0, i)
        for i in range(EARLY):
            multiply(early_banks[i], 1, i)
            finish(early_banks[i], i, parts=1)
        for i in range(EARLY, PIECES):
            bank = psum.tile([P, PIECE], F32, name="bank")
            for a in range(K_BLOCKS):
                multiply(bank, a, i)
            finish(bank, i, parts=(2 if i == PIECES - 1 else 1))
